import numpy as np
import ml_dtypes


def mxq(x, axis, fmt="e4m3"):
    dtype, down = {"e4m3": (ml_dtypes.float8_e4m3fn, 7), "e5m2": (ml_dtypes.float8_e5m2, 14)}[fmt]
    v = np.moveaxis(np.asarray(x, np.float32).astype(ml_dtypes.bfloat16).astype(np.float64), axis, -1)
    blocks = v.reshape(v.shape[:-1] + (-1, 32))
    amax = np.abs(blocks).max(-1, keepdims=True)
    byte = np.maximum(np.where(amax > 0, np.frexp(amax)[1] - 1 + 127, 0) - down, 1)
    scale = np.exp2(byte - 127.0)
    codes = (blocks / scale).astype(np.float32).astype(dtype).astype(np.float64)
    return np.moveaxis((codes * scale).reshape(v.shape), -1, axis)


WIDE = False


def mx_kscale(k):
    if not WIDE:
        return np.ones(k)
    levels = np.array([10, -10, 5, -5, 0])
    if k % 512:
        return np.exp2(np.random.permutation(np.resize(levels, k // 32))).repeat(32)
    a = np.empty((k // 512, 16))
    for p in range(k // 512):
        a[p, :8] = np.random.permutation(np.resize(levels, 8))
        for g in range(8):
            far = levels[np.abs(levels - a[p, g]) >= 10]
            a[p, g + 8] = far[np.random.randint(len(far))]
    return np.exp2(a.ravel()).repeat(32)


BF16 = ml_dtypes.bfloat16


def bf(x):
    return np.asarray(x, np.float32).astype(BF16)


def f64(x):
    return np.asarray(x).astype(np.float64)


B, K, D, H, C = 4096, 3, 512, 512, 256


def logsumexp(v, axis):
    m = np.max(v, axis=axis, keepdims=True)
    return m + np.log(np.sum(np.exp(v - m), axis=axis, keepdims=True))


def draw0():
    s, t = mx_kscale(D), mx_kscale(H)
    return {
        "x": bf(np.random.standard_normal((B, D)) * s),
        "r1": bf(1.0 + 0.5 * np.random.standard_normal((K, D))),
        "w1": bf(np.random.standard_normal((D, H)) / np.sqrt(D) / s[:, None]),
        "b1": bf(np.random.standard_normal((K, H)) * 0.3),
        "r2": bf(np.random.standard_normal((K, H)) * t),
        "w2": bf(np.random.standard_normal((H, C)) * 1.5 / np.sqrt(H) / t[:, None]),
    }


def core(x, r1, w1, b1, r2, w2):
    members = r1.shape[0]
    classes = w2.shape[1]
    xr = f64(x)[None, :, :] * f64(r1)[:, None, :]
    a = mxq(xr, 2, "e4m3") @ mxq(f64(w1), 0, "e4m3")
    h = np.maximum(a + f64(b1)[:, None, :], 0.0)
    hr = h * f64(r2)[:, None, :]
    logits = mxq(hr, 2, "e4m3") @ mxq(f64(w2), 0, "e4m3")
    lp = logits - logsumexp(logits, 2)
    mixed = np.squeeze(logsumexp(lp, 0), axis=0)
    return mixed - np.log(members) + np.log(classes)


def e4m3fn_bytes(y):
    return np.clip(np.asarray(y, np.float64), -448.0, 448.0).astype(np.float32).astype(ml_dtypes.float8_e4m3fn).view(np.uint8)


def e4m3fn_values(b):
    return np.asarray(b, np.uint8).view(ml_dtypes.float8_e4m3fn).astype(np.float64)


def setup_inputs():
    d = draw0()
    x0 = np.asarray(d['w1']).astype(np.float64)
    s = (np.max(np.abs(x0), axis=(1,), keepdims=True) / 448.0).astype(np.float32)
    out = {}
    for k, v in d.items():
        if k == 'w1':
            out['w1_bytes'] = e4m3fn_bytes(x0 / s.astype(np.float64))
            out['w1_scale'] = s
        else:
            out[k] = v
    return out


def reference(x, r1, w1_bytes, w1_scale, b1, r2, w2):
    return core(x, r1, e4m3fn_values(w1_bytes) * w1_scale.astype(np.float64), b1, r2, w2)

from contextlib import ExitStack
import math

import concourse.mybir as mybir
from concourse.masks import make_identity

F32 = mybir.dt.float32
BF16 = mybir.dt.bfloat16
U32 = mybir.dt.uint32
U8 = mybir.dt.uint8
FP8 = mybir.dt.float8_e4m3fn
FP8X4 = mybir.dt.float8_e4m3fn_x4
ALU = mybir.AluOpType
ACT = mybir.ActivationFunctionType

B, K, D, H, C = 4096, 3, 512, 512, 256
FLOPS = 2 * K * B * D * (H + C)

P = 128
PACK = 4
CHUNK = 512
TILES = CHUNK // P
CHUNKS = B // CHUNK
BASE = math.log(C) - math.log(K)

INT_ON_SCALAR = (0, 1)
LOG_STEPS = {4: (0, 1, 2), 7: (3, 4, 5), 8: (6, 7)}


def tile_tabmbatchensemblelogmeanprob_t_kernel(tc, x, r1, w1_bytes, w1_scale, b1, r2, w2, out):
    nc = tc.nc
    x_view = x.rearrange("(g p j) d -> g p j d", p=P, j=TILES)
    out_view = out.rearrange("(g p j) c -> g p j c", p=P, j=TILES)

    with ExitStack() as ctx:
        const = ctx.enter_context(tc.tile_pool(name="const", bufs=1))
        work = ctx.enter_context(tc.tile_pool(name="work", bufs=2))
        psum = ctx.enter_context(tc.psum_pool(name="psum", bufs=2))
        ctx.enter_context(tc.manual_schedule())

        r1_sb = const.tile([P, K, 2, 2], BF16, name="r1_sb")
        w1s_sb = const.tile([P, PACK], F32, name="w1s_sb")
        r2_sb = const.tile([P, K * PACK], BF16, name="r2_sb")
        b1_sb = const.tile([P, K * PACK], BF16, name="b1_sb")
        w1b_sb = const.tile([P, PACK, H], U8, name="w1b_sb")
        w2_sb = const.tile([P, PACK, C], BF16, name="w2_sb")

        xs = {}

        def load_x(g, parts):
            t = work.tile([P, TILES, D], BF16, name="x_sb", bufs=3, align_bytes=64)
            n = TILES // parts
            for i in range(parts):
                nc.sync.dma_start(out=t[:, i * n : (i + 1) * n, :], in_=x_view[g][:, i * n : (i + 1) * n, :])
            xs[g] = t

        nc.scalar.dma_start(out=w1s_sb[:], in_=w1_scale.rearrange("(p t) o -> p (t o)", t=PACK))
        nc.sync.dma_start(out=w1b_sb[:], in_=w1_bytes.rearrange("(p j) h -> p j h", j=PACK))
        nc.scalar.dma_start(
            out=r1_sb[:].rearrange("p k u e -> p k (u e)"), in_=r1.rearrange("k (p t) -> p k t", t=PACK)
        )
        load_x(0, 2)
        nc.scalar.dma_start(
            out=r2_sb[:].rearrange("p (k t) -> p k t", k=K), in_=r2.rearrange("k (p t) -> p k t", t=PACK)
        )
        nc.scalar.dma_start(
            out=b1_sb[:].rearrange("p (k t) -> p k t", k=K), in_=b1.rearrange("k (p t) -> p k t", t=PACK)
        )
        nc.sync.dma_start(out=w2_sb[:], in_=w2.rearrange("(p j) c -> p j c", j=PACK))
        load_x(1, 1)
        load_x(2, 1)

        ident = const.tile([P, P], F32, name="ident")
        make_identity(nc, ident[:])

        w1_wide = const.tile([P, PACK, H], BF16, name="w1_wide", align_bytes=64)
        for j in range(PACK):
            code = w1b_sb[:, j, :].bitcast(FP8)
            if j < 2:
                nc.scalar.activation(
                    out=w1_wide[:, j, :], in_=code, func=ACT.Copy, scale=w1s_sb[:, j : j + 1]
                )
            else:
                nc.vector.tensor_scalar(
                    out=w1_wide[:, j, :], in0=code, scalar1=w1s_sb[:, j : j + 1], scalar2=None, op0=ALU.mult
                )
        w1_grp = const.tile([P, H * PACK], BF16, name="w1_grp", align_bytes=64)
        nc.vector.tensor_copy(
            out=w1_grp[:].rearrange("p (t m j) -> p t m j", t=PACK, j=PACK),
            in_=w1_wide[:].rearrange("p j (m t) -> p t m j", t=PACK),
        )
        w1_codes = const.tile([P, H], U32, name="w1_codes", align_bytes=64)
        w1_planes = const.tile([P, H], U8, name="w1_planes", align_bytes=64)

        def quantize(codes, planes, grouped):
            nc.vector.quantize_mx(out=codes.bitcast(FP8X4), scales=planes, in_=grouped)

        xr, xc, xsc, hp, hi, hc, hsc = {}, {}, {}, {}, {}, {}, {}
        xt = {}
        n_sb, e_sb, s_sb, piv, negm, sums, rec, bdiff, cm, rho = {}, {}, {}, {}, {}, {}, {}, {}, {}, {}

        def transpose_x(g):
            for half in range(2):
                t = psum.tile([P, 2, 2 * P], F32, name="xt")
                xt[g, half] = t
                for jj in range(2):
                    words = xs[g][:, 2 * half + jj, :].bitcast(F32)
                    for u in range(2):
                        nc.tensor.transpose(
                            t[:, u, jj * P : (jj + 1) * P], words[:, u : D // 2 : 2], ident[:]
                        )

        def adapt(g, half):
            if half == 0:
                for k in range(K):
                    xr[g, k] = work.tile([P, CHUNK * PACK], BF16, name="xr%d" % k, align_bytes=64)
            words = xt[g, half][:].rearrange("p u n -> p (u n)").bitcast(BF16)
            src = words.rearrange("p (u n e) -> p n u e", u=2, e=2)
            for k in range(K):
                dst = xr[g, k][:, half * 1024 : (half + 1) * 1024]
                nc.vector.tensor_tensor(
                    out=dst.rearrange("p (n u e) -> p n u e", u=2, e=2),
                    in0=src,
                    in1=r1_sb[:, k].unsqueeze(1).to_broadcast([P, 2 * P, 2, 2]),
                    op=ALU.mult,
                )

        def quantize_x(g, k):
            xc[g, k] = work.tile([P, CHUNK], U32, name="xc%d" % k, align_bytes=64)
            xsc[g, k] = work.tile([P, CHUNK], U8, name="xsc%d" % k, align_bytes=64)
            quantize(xc[g, k][:], xsc[g, k][:], xr[g, k][:])

        def hidden(g, k):
            h = work.tile([P, PACK, CHUNK], BF16, name="hp%d" % k, bufs=1, align_bytes=64)
            hp[g, k] = h
            for t in range(PACK):
                a = psum.tile([P, CHUNK], F32, name="a", bufs=3)
                cols = slice(t * P, (t + 1) * P)
                nc.tensor.matmul_mx(
                    out=a[:],
                    lhsT=w1_codes[:, cols].bitcast(FP8X4),
                    lhsT_scale=w1_planes[:, cols],
                    rhs=xc[g, k][:].bitcast(FP8X4),
                    rhs_scale=xsc[g, k][:],
                    start=True,
                    stop=True,
                )
                i = k * PACK + t
                nc.scalar.activation(
                    out=h[:, t, :], in_=a[:], func=ACT.Relu, scale=r2_abs[:, i : i + 1], bias=b1_r2[:, i : i + 1]
                )

        def interleave(g, k):
            t = work.tile([P, CHUNK * PACK], BF16, name="hi%d" % k, bufs=1, align_bytes=64)
            hi[g, k] = t
            dst = t[:].rearrange("p (c i t) -> p c t i", i=4, t=PACK)
            src = hp[g, k][:].rearrange("p t (c i) -> p c t i", i=4)
            if k in INT_ON_SCALAR:
                nc.scalar.copy(out=dst, in_=src)
            else:
                nc.vector.tensor_copy(out=dst, in_=src)

        def quantize_h(g, k):
            hc[g, k] = work.tile([P, CHUNK], U32, name="hc%d" % k, align_bytes=64)
            hsc[g, k] = work.tile([P, CHUNK], U8, name="hsc%d" % k, align_bytes=64)
            quantize(hc[g, k][:], hsc[g, k][:], hi[g, k][:])

        def logits(g, half):
            if half == 0:
                n_sb[g] = work.tile([P, TILES, K, C], F32, name="n_sb")
                negm[g] = work.tile([P, TILES, K], F32, name="negm", bufs=3)
            for b in range(3):
                bank = psum.tile([P, 2, C], F32, name="l", bufs=3)
                for i in range(2):
                    unit = half * 6 + b * 2 + i
                    j, k = unit // K, unit % K
                    cols = slice(j * P, (j + 1) * P)
                    nc.tensor.matmul_mx(
                        out=bank[:, i, :],
                        lhsT=hc[g, k][:, cols].bitcast(FP8X4),
                        lhsT_scale=hsc[g, k][:, cols],
                        rhs=w2_codes[:, k, :].bitcast(FP8X4),
                        rhs_scale=w2_planes[:, k, :],
                        start=True,
                        stop=True,
                    )
                for i in range(2):
                    unit = half * 6 + b * 2 + i
                    j, k = unit // K, unit % K
                    nc.vector.tensor_scalar(
                        out=n_sb[g][:, j, k, :],
                        in0=bank[:, i, :],
                        scalar1=-1.0,
                        scalar2=None,
                        op0=ALU.mult,
                        op1=ALU.min,
                        accum_out=negm[g][:, j, k : k + 1],
                    )

        def exp_sums(g, half):
            if half == 0:
                sums[g] = work.tile([P, TILES, K], F32, name="sums", bufs=3)
            for j in (2 * half, 2 * half + 1):
                for k in range(K):
                    junk = work.tile([P, C], BF16, name="junk", bufs=2)
                    nc.scalar.activation(
                        out=junk[:],
                        in_=n_sb[g][:, j, k, :],
                        func=ACT.Exp,
                        scale=-1.0,
                        bias=negm[g][:, j, k : k + 1],
                        accum_out=sums[g][:, j, k : k + 1],
                    )

        def offsets(g):
            bdiff[g] = work.tile([P, TILES, 2], F32, name="bdiff", bufs=3)
            cm[g] = work.tile([P, TILES], F32, name="cm", bufs=5)
            nc.gpsimd.tensor_tensor(
                out=bdiff[g][:],
                in0=negm[g][:, :, 0:1].to_broadcast([P, TILES, 2]),
                in1=negm[g][:, :, 1:3],
                op=ALU.subtract,
            )
            nc.gpsimd.tensor_scalar(
                out=cm[g][:], in0=negm[g][:, :, 0], scalar1=BASE, scalar2=1.0, op0=ALU.add, op1=ALU.mult
            )

        def pivots(g):
            piv[g] = work.tile([P, TILES, C], F32, name="piv", bufs=5)
            for k in (1, 2):
                for j in range(TILES):
                    nc.vector.scalar_tensor_tensor(
                        out=piv[g][:, j, :],
                        in0=n_sb[g][:, j, k, :],
                        scalar=bdiff[g][:, j, k - 1 : k],
                        in1=n_sb[g][:, j, 0, :] if k == 1 else piv[g][:, j, :],
                        op0=ALU.add,
                        op1=ALU.min,
                    )

        def distances(g):
            e_sb[g] = work.tile([P, TILES, K, C], F32, name="e_sb")
            nc.vector.tensor_tensor(
                out=e_sb[g][:, :, 0, :], in0=n_sb[g][:, :, 0, :], in1=piv[g][:], op=ALU.subtract
            )
            for j in range(TILES):
                for k in (1, 2):
                    nc.vector.scalar_tensor_tensor(
                        out=e_sb[g][:, j, k, :],
                        in0=n_sb[g][:, j, k, :],
                        scalar=bdiff[g][:, j, k - 1 : k],
                        in1=piv[g][:, j, :],
                        op0=ALU.add,
                        op1=ALU.subtract,
                    )

        def exps(g):
            for j in range(TILES):
                t = e_sb[g][:, j].rearrange("p k c -> p (k c)")
                nc.scalar.activation(out=t, in_=t, func=ACT.Exp, scale=-1.0)

        def weights(g):
            rec[g] = work.tile([P, TILES, K], F32, name="rec", bufs=5)
            rho[g] = work.tile([P, TILES, 2], F32, name="rho", bufs=3)
            nc.vector.reciprocal(out=rec[g][:], in_=sums[g][:])
            nc.gpsimd.tensor_tensor(
                out=rho[g][:],
                in0=sums[g][:, :, 0:1].to_broadcast([P, TILES, 2]),
                in1=rec[g][:, :, 1:3],
                op=ALU.mult,
            )

        def mix(g):
            s_sb[g] = work.tile([P, TILES, C], F32, name="s_sb", bufs=5)
            for k in (1, 2):
                for j in range(TILES):
                    nc.vector.scalar_tensor_tensor(
                        out=s_sb[g][:, j, :],
                        in0=e_sb[g][:, j, k, :],
                        scalar=rho[g][:, j, k - 1 : k],
                        in1=e_sb[g][:, j, 0, :] if k == 1 else s_sb[g][:, j, :],
                        op0=ALU.mult,
                        op1=ALU.add,
                    )

        def logs(g, j):
            nc.scalar.activation(
                out=s_sb[g][:, j, :], in_=s_sb[g][:, j, :], func=ACT.Ln, scale=rec[g][:, j, 0:1]
            )

        def finish(g):
            for j in range(TILES):
                nc.vector.scalar_tensor_tensor(
                    out=s_sb[g][:, j, :],
                    in0=s_sb[g][:, j, :],
                    scalar=cm[g][:, j : j + 1],
                    in1=piv[g][:, j, :],
                    op0=ALU.add,
                    op1=ALU.subtract,
                )
            nc.sync.dma_start(out=out_view[g], in_=s_sb[g][:])

        transpose_x(0)
        adapt(0, 0)
        quantize(w1_codes[:], w1_planes[:], w1_grp[:])
        adapt(0, 1)
        for k in range(K):
            quantize_x(0, k)
        r2_abs = const.tile([P, K * PACK], F32, name="r2_abs")
        b1_r2 = const.tile([P, K * PACK], F32, name="b1_r2")
        sgn01 = const.tile([P, K * PACK], F32, name="sgn01")
        sgn = const.tile([P, K, PACK], BF16, name="sgn")
        nc.vector.scalar_tensor_tensor(
            out=r2_abs[:], in0=r2_sb[:], scalar=-1.0, in1=r2_sb[:], op0=ALU.mult, op1=ALU.max
        )
        nc.vector.tensor_scalar(
            out=sgn01[:], in0=r2_sb[:], scalar1=0.0, scalar2=2.0, op0=ALU.is_ge, op1=ALU.mult
        )
        nc.vector.tensor_tensor(out=b1_r2[:], in0=r2_abs[:], in1=b1_sb[:], op=ALU.mult)
        nc.vector.tensor_scalar(
            out=sgn[:].rearrange("p k t -> p (k t)"), in0=sgn01[:], scalar1=-1.0, scalar2=None, op0=ALU.add
        )
        w2_grp = const.tile([P, C, PACK], BF16, name="w2_grp", align_bytes=64)
        w2_signed = const.tile([P, K, C * PACK], BF16, name="w2_signed", align_bytes=64)
        w2_codes = const.tile([P, K, C], U32, name="w2_codes", align_bytes=64)
        w2_planes = const.tile([P, K, C], U8, name="w2_planes", align_bytes=64)
        nc.scalar.copy(out=w2_grp[:], in_=w2_sb[:].rearrange("p j c -> p c j"))

        def sign_w2(k):
            nc.vector.tensor_tensor(
                out=w2_signed[:, k, :].rearrange("p (c j) -> p c j", j=PACK),
                in0=w2_grp[:],
                in1=sgn[:, k, :].unsqueeze(1).to_broadcast([P, C, PACK]),
                op=ALU.mult,
            )

        for step in range(-1, CHUNKS + 1):
            gx, gf, gl, gs = step + 2, step + 1, step, step - 1
            if 3 <= step + 4 < CHUNKS:
                load_x(step + 4, 1)
            do_x = gx < CHUNKS
            do_f = gf < CHUNKS
            do_l = 0 <= gl < CHUNKS
            do_s = 0 <= gs < CHUNKS
            logged = [(g, j) for g in LOG_STEPS.get(step, ()) for j in range(TILES)]
            early = logged if step < CHUNKS else []
            if do_x:
                transpose_x(gx)
            if do_s:
                exps(gs)
                weights(gs)
            if do_l:
                logits(gl, 0)
            if do_x:
                adapt(gx, 0)
            if do_f:
                hidden(gf, 0)
            for g, j in early[: len(early) // 2]:
                logs(g, j)
            if do_l:
                logits(gl, 1)
                offsets(gl)
            if do_f:
                hidden(gf, 1)
            for g, j in early[len(early) // 2 :]:
                logs(g, j)
            if do_x:
                adapt(gx, 1)
            if do_l:
                exp_sums(gl, 0)
                pivots(gl)
            if do_f:
                interleave(gf, 0)
            if do_l:
                exp_sums(gl, 1)
                distances(gl)
            if do_f:
                hidden(gf, 2)
            if do_x:
                for k in range(K):
                    quantize_x(gx, k)
            if do_f:
                interleave(gf, 1)
            if do_s:
                mix(gs)
            if step == -1:
                for k in range(K):
                    sign_w2(k)
                for k in range(K):
                    quantize(w2_codes[:, k, :], w2_planes[:, k, :], w2_signed[:, k, :])
            if step >= CHUNKS:
                for g, j in logged:
                    logs(g, j)
            for g in LOG_STEPS.get(step, ()):
                finish(g)
            if do_f:
                interleave(gf, 2)
                for k in range(K):
                    quantize_h(gf, k)
